import numpy as np
import ml_dtypes


def mxq(x, axis, fmt="e4m3"):
    dtype, down = {"e4m3": (ml_dtypes.float8_e4m3fn, 7), "e5m2": (ml_dtypes.float8_e5m2, 14)}[fmt]
    v = np.moveaxis(np.asarray(x, np.float32).astype(ml_dtypes.bfloat16).astype(np.float64), axis, -1)
    blocks = v.reshape(v.shape[:-1] + (-1, 32))
    amax = np.abs(blocks).max(-1, keepdims=True)
    byte = np.maximum(np.where(amax > 0, np.frexp(amax)[1] - 1 + 127, 0) - down, 1)
    scale = np.exp2(byte - 127.0)
    codes = (blocks / scale).astype(np.float32).astype(dtype).astype(np.float64)
    return np.moveaxis((codes * scale).reshape(v.shape), -1, axis)


WIDE = False


def mx_kscale(k):
    if not WIDE:
        return np.ones(k)
    levels = np.array([30, -30])
    if k % 512:
        return np.exp2(np.random.permutation(np.resize(levels, k // 32))).repeat(32)
    a = np.empty((k // 512, 16))
    for p in range(k // 512):
        a[p, :8] = np.random.permutation(np.resize(levels, 8))
        for g in range(8):
            far = levels[np.abs(levels - a[p, g]) >= 10]
            a[p, g + 8] = far[np.random.randint(len(far))]
    return np.exp2(a.ravel()).repeat(32)


BF16 = ml_dtypes.bfloat16


def bf(x):
    return np.asarray(x, np.float32).astype(BF16)


def f64(x):
    return np.asarray(x).astype(np.float64)


X, Y, C = 1024, 1536, 512


def setup_inputs():
    s, t, u = mx_kscale(X), mx_kscale(C), mx_kscale(Y)
    d_x = np.random.standard_normal((X, X)) / np.sqrt(X)
    psi = np.random.standard_normal((X, Y))
    background = np.random.standard_normal((X, C))
    d_coarse = np.random.standard_normal((C, Y)) / np.sqrt(C)
    cores = np.random.standard_normal((X, Y)) * np.exp(np.random.standard_normal((X, Y)) - 1.0)
    d_fine = np.random.standard_normal((Y, Y)) / np.sqrt(Y)
    return {"d_x": bf(d_x * s),
            "psi": bf(psi / s[:, None]),
            "background": bf(background * t),
            "d_coarse": bf(d_coarse / t[:, None]),
            "cores": bf(cores * u),
            "d_fine": bf(d_fine / u[:, None]),
            "beta": bf(0.4 * np.random.standard_normal(Y))}


def reference(d_x, psi, background, d_coarse, cores, d_fine, beta):
    v = mxq(f64(d_x), 1, "e4m3") @ mxq(f64(psi), 0, "e4m3")
    smooth = mxq(f64(background), 1, "e4m3")
    rough = mxq(f64(cores), 1, "e5m2")
    zeta_y = (smooth @ mxq(f64(d_coarse), 0, "e4m3")) + (rough @ mxq(f64(d_fine), 0, "e4m3"))
    return v * (zeta_y + f64(beta))

@@ -1,0 +1,355 @@
+from contextlib import ExitStack
+
+import concourse.mybir as mybir
+from concourse.masks import make_identity
+
+X, Y, C = 1024, 1536, 512
+FLOPS = 2 * X * Y * (X + C + Y)
+
+F32 = mybir.dt.float32
+BF16 = mybir.dt.bfloat16
+U32 = mybir.dt.uint32
+U8 = mybir.dt.uint8
+E4M3 = mybir.dt.float8_e4m3fn_x4
+E5M2 = mybir.dt.float8_e5m2_x4
+ADD = mybir.AluOpType.add
+MULT = mybir.AluOpType.mult
+
+P = 128
+PACK = 4
+K_PASS = P * PACK
+N_TILE = 512
+ROW_TILES = X // P
+CHUNKS = Y // N_TILE
+ZETA_PASSES = (0, 1, 2, 3)
+V_PASSES = (4, 5)
+EARLY_VECTOR_COLS = 512
+MID_VECTOR_COLS = 128
+LATE_VECTOR_COLS = 32
+WARM = (7, 2, 8)
+WARM_N = 256
+RAW_BUFS = 8
+
+
+def tile_meridional_vorticity_advection_s2_kernel(
+    tc, d_x, psi, background, d_coarse, cores, d_fine, beta, out
+):
+    nc = tc.nc
+    left_of = [(background, 0, E4M3), (cores, 0, E5M2), (cores, 1, E5M2), (cores, 2, E5M2), (d_x, 0, E4M3), (d_x, 1, E4M3)]
+    right_of = [(d_coarse, 0), (d_fine, 0), (d_fine, 1), (d_fine, 2), (psi, 0), (psi, 1)]
+    out_rows = out.rearrange("(p i) y -> p i y", i=ROW_TILES)
+
+    with ExitStack() as ctx:
+        keep = ctx.enter_context(tc.tile_pool(name="keep", bufs=1))
+        stream = ctx.enter_context(tc.tile_pool(name="stream", bufs=1))
+        psum = ctx.enter_context(tc.psum_pool(name="psum", bufs=1))
+        ctx.enter_context(tc.manual_schedule(engines={mybir.EngineType.PE, mybir.EngineType.SP}))
+
+        free_banks = list(range(8))
+        left_raw, left_grouped, left_mx = {}, {}, {}
+        right_raw, right_grouped, right_mx = {}, {}, {}
+        open_banks, shifted = {}, {}
+
+        def take_bank(shape):
+            b = free_banks.pop(0)
+            return b, psum.tile(shape, F32, name="bank%d" % b)
+
+        ident = keep.tile([P, P], F32, name="ident")
+        make_identity(nc, ident[:])
+        beta_cols = keep.tile([P, 2, 6], BF16, name="beta_cols")
+        beta_row = keep.tile([P, Y], BF16, name="beta_row")
+
+        def load_beta():
+            nc.sync.dma_start(out=beta_cols[:], in_=beta.rearrange("(h p c) -> p h c", h=2, c=6))
+
+        def spread_beta():
+            words = beta_cols[:].rearrange("p h c -> p (h c)").bitcast(F32)
+            row_words = beta_row[:].bitcast(F32)
+            for h in range(2):
+                b, bank = take_bank([P, 3, P])
+                for c in range(3):
+                    column = words[:, 3 * h + c : 3 * h + c + 1].to_broadcast([P, P])
+                    nc.tensor.transpose(bank[:, c, :], column, ident[:])
+                nc.scalar.copy(
+                    out=row_words[:, 3 * P * h : 3 * P * (h + 1)].rearrange("p (n c) -> p n c", c=3),
+                    in_=bank[:].rearrange("p c n -> p n c"),
+                )
+                free_banks.append(b)
+
+        def load_left(first_pass, pairs):
+            matrix = left_of[first_pass][0]
+            k = matrix.shape[1]
+            rows = matrix.rearrange("(p i) k -> p (i k)", i=ROW_TILES)
+            raw = keep.tile([P, 2 * k * len(pairs)], BF16, name="left_raw%d_%d" % (first_pass, pairs[0]))
+            nc.sync.dma_start(out=raw[:], in_=rows[:, 2 * k * pairs[0] : 2 * k * (pairs[-1] + 1)])
+            for n, pair in enumerate(pairs):
+                for g in range(k // K_PASS):
+                    left_raw[first_pass + g, pair] = (raw[:].bitcast(F32), n * k + g * (K_PASS // 2), k // 2)
+
+        def turn_left(g, pair):
+            words, first, tile_words = left_raw[g, pair]
+            b, bank = take_bank([P, 2, 2, P])
+            for s in range(2):
+                for u in range(2):
+                    w0 = first + s * tile_words
+                    nc.tensor.transpose(bank[:, s, u, :], words[:, w0 + u : w0 + K_PASS // 2 : 2], ident[:])
+            grouped = stream.tile([P, 2 * K_PASS], BF16, name="left_grouped", bufs=4, align_bytes=64)
+            nc.scalar.copy(
+                out=grouped[:].bitcast(F32).rearrange("p (s r u) -> p s r u", s=2, u=2),
+                in_=bank[:].rearrange("p s u r -> p s r u"),
+            )
+            free_banks.append(b)
+            left_grouped[g, pair] = grouped
+
+        def quantize_left(g, pair):
+            codes = keep.tile([P, 2 * P], U32, name="left_codes%d_%d" % (g, pair), align_bytes=64)
+            scales = keep.tile([P, 2 * P], U8, name="left_scales%d_%d" % (g, pair), align_bytes=64)
+            nc.vector.quantize_mx(out=codes[:].bitcast(left_of[g][2]), scales=scales[:], in_=left_grouped[g, pair][:])
+            left_mx[g, pair] = (codes, scales)
+
+        def load_right(g, j):
+            matrix, part = right_of[g]
+            rows = matrix[part * K_PASS : (part + 1) * K_PASS, j * N_TILE : (j + 1) * N_TILE]
+            raw = stream.tile([P, PACK, N_TILE], BF16, name="right_raw", bufs=RAW_BUFS)
+            nc.sync.dma_start(out=raw[:], in_=rows.rearrange("(p t) n -> p t n", t=PACK))
+            right_raw[g, j] = raw
+
+        def group_right(g, j, vector_cols):
+            raw = right_raw[g, j]
+            grouped = stream.tile([P, N_TILE, PACK], BF16, name="right_grouped", bufs=4, align_bytes=64)
+            split = N_TILE - vector_cols
+            if split > 0:
+                nc.scalar.copy(
+                    out=grouped[:, :split, :].rearrange("p (c i) t -> p c t i", i=4),
+                    in_=raw[:, :, :split].rearrange("p t (c i) -> p c t i", i=4),
+                )
+            if vector_cols > 0:
+                nc.vector.tensor_copy(
+                    out=grouped[:, split:, :].rearrange("p (c i) t -> p c t i", i=4),
+                    in_=raw[:, :, split:].rearrange("p t (c i) -> p c t i", i=4),
+                )
+            right_grouped[g, j] = grouped
+
+        def quantize_right(g, j):
+            codes = keep.tile([P, N_TILE], U32, name="right_codes%d_%d" % (g, j), align_bytes=64)
+            scales = keep.tile([P, N_TILE], U8, name="right_scales%d_%d" % (g, j), align_bytes=64)
+            nc.vector.quantize_mx(
+                out=codes[:].bitcast(E4M3),
+                scales=scales[:],
+                in_=right_grouped[g, j][:].rearrange("p n t -> p (n t)"),
+            )
+            right_mx[g, j] = (codes, scales)
+
+        def multiply(g, i, j):
+            passes = ZETA_PASSES if g in ZETA_PASSES else V_PASSES
+            if g == passes[0]:
+                open_banks[i] = take_bank([P, N_TILE])
+            left_codes, left_scales = left_mx[g, i // 2]
+            right_codes, right_scales = right_mx[g, j]
+            cols = slice(P * (i % 2), P * (i % 2 + 1))
+            nc.tensor.matmul_mx(
+                out=open_banks[i][1][:],
+                lhsT=left_codes[:, cols].bitcast(left_of[g][2]),
+                lhsT_scale=left_scales[:, cols],
+                rhs=right_codes[:].bitcast(E4M3),
+                rhs_scale=right_scales[:],
+                start=(g == passes[0]),
+                stop=(g == passes[-1]),
+            )
+
+        def add_beta(i, j):
+            b, bank = open_banks[i]
+            shifted[i] = stream.tile([P, N_TILE], F32, name="shifted", bufs=14)
+            nc.vector.tensor_tensor(
+                out=shifted[i][:], in0=bank[:], in1=beta_row[:, j * N_TILE : (j + 1) * N_TILE], op=ADD
+            )
+            free_banks.append(b)
+
+        def finish(i, j):
+            b, bank = open_banks[i]
+            nc.vector.tensor_tensor(out=shifted[i][:], in0=bank[:], in1=shifted[i][:], op=MULT)
+            free_banks.append(b)
+            nc.sync.dma_start(out=out_rows[:, i, j * N_TILE : (j + 1) * N_TILE], in_=shifted[i][:])
+
+        warm_in = keep.tile([P, PACK * WARM_N], BF16, name="warm_in", align_bytes=64)
+        warm_codes = keep.tile([P, WARM_N], U32, name="warm_codes", align_bytes=64)
+        warm_scales = keep.tile([P, WARM_N], U8, name="warm_scales", align_bytes=64)
+
+        def warm_up(count):
+            if count == 0:
+                return
+            b, bank = take_bank([P, WARM_N])
+            for n in range(count):
+                nc.tensor.matmul_mx(
+                    out=bank[:],
+                    lhsT=warm_codes[:, :P].bitcast(E4M3),
+                    lhsT_scale=warm_scales[:, :P],
+                    rhs=warm_codes[:].bitcast(E4M3),
+                    rhs_scale=warm_scales[:],
+                    start=True,
+                    stop=True,
+                )
+            free_banks.append(b)
+
+        if sum(WARM):
+            nc.vector.memset(warm_in[:].bitcast(U32), 0)
+            nc.vector.quantize_mx(out=warm_codes[:].bitcast(E4M3), scales=warm_scales[:], in_=warm_in[:])
+
+        low, high = range(0, 4), range(4, 8)
+
+        def sweep(g, tiles, j):
+            for i in tiles:
+                multiply(g, i, j)
+
+        load_left(0, [0, 1])
+        load_beta()
+        load_left(1, [0])
+        load_right(0, 0)
+        load_left(1, [1])
+        load_right(1, 0)
+        load_left(0, [2, 3])
+        load_right(2, 0)
+        load_left(1, [2])
+        load_right(3, 0)
+        load_left(1, [3])
+        load_right(4, 0)
+        load_left(4, [0])
+        load_left(4, [1])
+        load_right(5, 0)
+        load_left(4, [2])
+        load_left(4, [3])
+
+        later = [(g, j) for j in range(1, CHUNKS) for g in range(6)]
+        to_load = list(later)
+        to_group = [(4, 0), (5, 0)] + later
+        to_quantize = list(to_group)
+
+        def next_load():
+            if to_load:
+                load_right(*to_load.pop(0))
+
+        def next_group(cols):
+            if to_group:
+                group_right(*to_group.pop(0), cols)
+                next_load()
+
+        def next_quantize():
+            if to_quantize:
+                quantize_right(*to_quantize.pop(0))
+
+        def tile_passes(passes, i, j):
+            for g in passes:
+                multiply(g, i, j)
+
+        def turn_all(passes, pair):
+            for g in passes:
+                turn_left(g, pair)
+
+        def quantize_all(passes, pair):
+            for g in passes:
+                quantize_left(g, pair)
+
+        for n in range(RAW_BUFS - 6):
+            next_load()
+
+        warm_up(WARM[0])
+        turn_left(0, 0)
+        turn_left(0, 1)
+        spread_beta()
+        warm_up(WARM[1])
+        quantize_left(0, 0)
+        quantize_left(0, 1)
+        turn_all((1, 2, 3), 0)
+        warm_up(WARM[2])
+        quantize_left(1, 0)
+        group_right(0, 0, EARLY_VECTOR_COLS)
+        next_load()
+        quantize_left(2, 0)
+        quantize_right(0, 0)
+        quantize_left(3, 0)
+        turn_all((1, 2, 3), 1)
+        sweep(0, low, 0)
+        quantize_left(1, 1)
+        group_right(1, 0, EARLY_VECTOR_COLS)
+        next_load()
+        quantize_left(2, 1)
+        quantize_right(1, 0)
+        quantize_left(3, 1)
+        turn_left(0, 2)
+        turn_left(0, 3)
+        sweep(1, low, 0)
+        group_right(2, 0, EARLY_VECTOR_COLS)
+        next_load()
+        quantize_left(0, 2)
+        quantize_right(2, 0)
+        quantize_left(0, 3)
+        turn_all((1, 2, 3), 2)
+        sweep(2, low, 0)
+        quantize_left(1, 2)
+        group_right(3, 0, EARLY_VECTOR_COLS)
+        next_load()
+        quantize_left(2, 2)
+        quantize_right(3, 0)
+        quantize_left(3, 2)
+        turn_all((1, 2, 3), 3)
+        sweep(3, low, 0)
+        quantize_left(1, 3)
+        quantize_left(2, 3)
+        next_group(MID_VECTOR_COLS)
+        quantize_left(3, 3)
+        add_beta(0, 0)
+        add_beta(1, 0)
+        for i in (4, 5):
+            tile_passes(ZETA_PASSES, i, 0)
+        next_quantize()
+        add_beta(2, 0)
+        add_beta(3, 0)
+        turn_all(V_PASSES, 0)
+        turn_all(V_PASSES, 1)
+        next_group(MID_VECTOR_COLS)
+        add_beta(4, 0)
+        add_beta(5, 0)
+        for i in (6, 7):
+            tile_passes(ZETA_PASSES, i, 0)
+        quantize_all(V_PASSES, 0)
+        quantize_all(V_PASSES, 1)
+        next_quantize()
+        turn_all(V_PASSES, 2)
+        turn_all(V_PASSES, 3)
+        next_group(MID_VECTOR_COLS)
+        add_beta(6, 0)
+        add_beta(7, 0)
+        for i in low:
+            tile_passes(V_PASSES, i, 0)
+        quantize_all(V_PASSES, 2)
+        quantize_all(V_PASSES, 3)
+        next_quantize()
+        next_group(MID_VECTOR_COLS)
+        for i in high:
+            tile_passes(V_PASSES, i, 0)
+            finish(i - 4, 0)
+            if i % 2 == 1:
+                next_quantize()
+                next_group(MID_VECTOR_COLS)
+
+        for j in range(1, CHUNKS):
+            for g in ZETA_PASSES:
+                sweep(g, low, j)
+                finish(4 + g, j - 1)
+                if g % 2 == 0:
+                    next_quantize()
+                    next_group(LATE_VECTOR_COLS)
+            for i in low:
+                tile_passes(ZETA_PASSES, 4 + i, j)
+                add_beta(i, j)
+                if i > 0:
+                    tile_passes(V_PASSES, i - 1, j)
+                    add_beta(3 + i, j)
+                    finish(i - 1, j)
+                next_quantize()
+                next_group(LATE_VECTOR_COLS)
+            add_beta(7, j)
+            for i in (3, 4, 5, 6, 7):
+                tile_passes(V_PASSES, i, j)
+                if i == 3 or j == CHUNKS - 1:
+                    finish(i, j)

@@ -24,8 +24,8 @@ CHUNKS = Y // N_TILE
 ZETA_PASSES = (0, 1, 2, 3)
 V_PASSES = (4, 5)
 EARLY_VECTOR_COLS = 512
-MID_VECTOR_COLS = 128
-LATE_VECTOR_COLS = 32
+MID_VECTOR_COLS = 160
+LATE_VECTOR_COLS = 0
 WARM = (7, 2, 8)
 WARM_N = 256
 RAW_BUFS = 8
@@ -43,7 +43,7 @@ def tile_meridional_vorticity_advection_s2_kernel(
         keep = ctx.enter_context(tc.tile_pool(name="keep", bufs=1))
         stream = ctx.enter_context(tc.tile_pool(name="stream", bufs=1))
         psum = ctx.enter_context(tc.psum_pool(name="psum", bufs=1))
-        ctx.enter_context(tc.manual_schedule(engines={mybir.EngineType.PE, mybir.EngineType.SP}))
+        ctx.enter_context(tc.manual_schedule())
 
         free_banks = list(range(8))
         left_raw, left_grouped, left_mx = {}, {}, {}
@@ -86,26 +86,35 @@ def tile_meridional_vorticity_advection_s2_kernel(
                 for g in range(k // K_PASS):
                     left_raw[first_pass + g, pair] = (raw[:].bitcast(F32), n * k + g * (K_PASS // 2), k // 2)
 
-        def turn_left(g, pair):
-            words, first, tile_words = left_raw[g, pair]
-            b, bank = take_bank([P, 2, 2, P])
-            for s in range(2):
-                for u in range(2):
-                    w0 = first + s * tile_words
-                    nc.tensor.transpose(bank[:, s, u, :], words[:, w0 + u : w0 + K_PASS // 2 : 2], ident[:])
-            grouped = stream.tile([P, 2 * K_PASS], BF16, name="left_grouped", bufs=4, align_bytes=64)
-            nc.scalar.copy(
-                out=grouped[:].bitcast(F32).rearrange("p (s r u) -> p s r u", s=2, u=2),
-                in_=bank[:].rearrange("p s u r -> p s r u"),
-            )
-            free_banks.append(b)
-            left_grouped[g, pair] = grouped
+        def turn_left(*units):
+            grouped = stream.tile([P, 4 * K_PASS], BF16, name="left_grouped", bufs=4, align_bytes=64)
+            for n, (g, pair) in enumerate(units):
+                words, first, tile_words = left_raw[g, pair]
+                b, bank = take_bank([P, 2, 2, P])
+                for s in range(2):
+                    for u in range(2):
+                        w0 = first + s * tile_words
+                        nc.tensor.transpose(bank[:, s, u, :], words[:, w0 + u : w0 + K_PASS // 2 : 2], ident[:])
+                nc.scalar.copy(
+                    out=grouped[:, 2 * K_PASS * n : 2 * K_PASS * (n + 1)]
+                    .bitcast(F32)
+                    .rearrange("p (s r u) -> p s r u", s=2, u=2),
+                    in_=bank[:].rearrange("p s u r -> p s r u"),
+                )
+                free_banks.append(b)
+            left_grouped[units] = grouped
 
-        def quantize_left(g, pair):
-            codes = keep.tile([P, 2 * P], U32, name="left_codes%d_%d" % (g, pair), align_bytes=64)
-            scales = keep.tile([P, 2 * P], U8, name="left_scales%d_%d" % (g, pair), align_bytes=64)
-            nc.vector.quantize_mx(out=codes[:].bitcast(left_of[g][2]), scales=scales[:], in_=left_grouped[g, pair][:])
-            left_mx[g, pair] = (codes, scales)
+        def quantize_left(*units):
+            width = 2 * P * len(units)
+            codes = keep.tile([P, width], U32, name="left_codes%d_%d" % units[0], align_bytes=64)
+            scales = keep.tile([P, width], U8, name="left_scales%d_%d" % units[0], align_bytes=64)
+            nc.vector.quantize_mx(
+                out=codes[:].bitcast(left_of[units[0][0]][2]),
+                scales=scales[:],
+                in_=left_grouped[units][:, : PACK * width],
+            )
+            for n, unit in enumerate(units):
+                left_mx[unit] = (codes, scales, 2 * P * n)
 
         def load_right(g, j):
             matrix, part = right_of[g]
@@ -144,9 +153,9 @@ def tile_meridional_vorticity_advection_s2_kernel(
             passes = ZETA_PASSES if g in ZETA_PASSES else V_PASSES
             if g == passes[0]:
                 open_banks[i] = take_bank([P, N_TILE])
-            left_codes, left_scales = left_mx[g, i // 2]
+            left_codes, left_scales, first = left_mx[g, i // 2]
             right_codes, right_scales = right_mx[g, j]
-            cols = slice(P * (i % 2), P * (i % 2 + 1))
+            cols = slice(first + P * (i % 2), first + P * (i % 2 + 1))
             nc.tensor.matmul_mx(
                 out=open_banks[i][1][:],
                 lhsT=left_codes[:, cols].bitcast(left_of[g][2]),
@@ -159,7 +168,7 @@ def tile_meridional_vorticity_advection_s2_kernel(
 
         def add_beta(i, j):
             b, bank = open_banks[i]
-            shifted[i] = stream.tile([P, N_TILE], F32, name="shifted", bufs=14)
+            shifted[i] = stream.tile([P, N_TILE], F32, name="shifted", bufs=12)
             nc.vector.tensor_tensor(
                 out=shifted[i][:], in0=bank[:], in1=beta_row[:, j * N_TILE : (j + 1) * N_TILE], op=ADD
             )
@@ -213,9 +222,9 @@ def tile_meridional_vorticity_advection_s2_kernel(
         load_right(3, 0)
         load_left(1, [3])
         load_right(4, 0)
+        load_right(5, 0)
         load_left(4, [0])
         load_left(4, [1])
-        load_right(5, 0)
         load_left(4, [2])
         load_left(4, [3])
 
@@ -241,115 +250,123 @@ def tile_meridional_vorticity_advection_s2_kernel(
             for g in passes:
                 multiply(g, i, j)
 
-        def turn_all(passes, pair):
-            for g in passes:
-                turn_left(g, pair)
-
-        def quantize_all(passes, pair):
-            for g in passes:
-                quantize_left(g, pair)
+        def turn_cores(pair):
+            turn_left((1, pair), (2, pair))
+            turn_left((3, pair))
 
         for n in range(RAW_BUFS - 6):
             next_load()
 
         warm_up(WARM[0])
-        turn_left(0, 0)
-        turn_left(0, 1)
+        turn_left((0, 0), (0, 1))
         spread_beta()
         warm_up(WARM[1])
-        quantize_left(0, 0)
-        quantize_left(0, 1)
-        turn_all((1, 2, 3), 0)
+        quantize_left((0, 0), (0, 1))
+        turn_cores(0)
         warm_up(WARM[2])
-        quantize_left(1, 0)
         group_right(0, 0, EARLY_VECTOR_COLS)
         next_load()
-        quantize_left(2, 0)
+        quantize_left((1, 0), (2, 0))
         quantize_right(0, 0)
-        quantize_left(3, 0)
-        turn_all((1, 2, 3), 1)
+        quantize_left((3, 0))
+        turn_cores(1)
         sweep(0, low, 0)
-        quantize_left(1, 1)
         group_right(1, 0, EARLY_VECTOR_COLS)
         next_load()
-        quantize_left(2, 1)
+        quantize_left((1, 1), (2, 1))
         quantize_right(1, 0)
-        quantize_left(3, 1)
-        turn_left(0, 2)
-        turn_left(0, 3)
+        quantize_left((3, 1))
+        turn_left((0, 2), (0, 3))
         sweep(1, low, 0)
         group_right(2, 0, EARLY_VECTOR_COLS)
         next_load()
-        quantize_left(0, 2)
+        quantize_left((0, 2), (0, 3))
         quantize_right(2, 0)
-        quantize_left(0, 3)
-        turn_all((1, 2, 3), 2)
+        turn_cores(2)
         sweep(2, low, 0)
-        quantize_left(1, 2)
         group_right(3, 0, EARLY_VECTOR_COLS)
         next_load()
-        quantize_left(2, 2)
+        quantize_left((1, 2), (2, 2))
         quantize_right(3, 0)
-        quantize_left(3, 2)
-        turn_all((1, 2, 3), 3)
+        quantize_left((3, 2))
+        turn_cores(3)
         sweep(3, low, 0)
-        quantize_left(1, 3)
-        quantize_left(2, 3)
         next_group(MID_VECTOR_COLS)
-        quantize_left(3, 3)
         add_beta(0, 0)
+        quantize_left((1, 3), (2, 3))
         add_beta(1, 0)
+        quantize_left((3, 3))
         for i in (4, 5):
             tile_passes(ZETA_PASSES, i, 0)
-        next_quantize()
         add_beta(2, 0)
         add_beta(3, 0)
-        turn_all(V_PASSES, 0)
-        turn_all(V_PASSES, 1)
+        next_quantize()
         next_group(MID_VECTOR_COLS)
+        turn_left((4, 0), (5, 0))
+        turn_left((4, 1), (5, 1))
         add_beta(4, 0)
         add_beta(5, 0)
         for i in (6, 7):
             tile_passes(ZETA_PASSES, i, 0)
-        quantize_all(V_PASSES, 0)
-        quantize_all(V_PASSES, 1)
         next_quantize()
-        turn_all(V_PASSES, 2)
-        turn_all(V_PASSES, 3)
+        quantize_left((4, 0), (5, 0))
         next_group(MID_VECTOR_COLS)
+        quantize_left((4, 1), (5, 1))
         add_beta(6, 0)
         add_beta(7, 0)
-        for i in low:
-            tile_passes(V_PASSES, i, 0)
-        quantize_all(V_PASSES, 2)
-        quantize_all(V_PASSES, 3)
         next_quantize()
         next_group(MID_VECTOR_COLS)
+        turn_left((4, 2), (5, 2))
+        turn_left((4, 3), (5, 3))
+        for i in low:
+            tile_passes(V_PASSES, i, 0)
+        next_quantize()
+        next_group(MID_VECTOR_COLS)
+        finish(0, 0)
+        quantize_left((4, 2), (5, 2))
+        finish(1, 0)
+        quantize_left((4, 3), (5, 3))
+        finish(2, 0)
+        finish(3, 0)
         for i in high:
             tile_passes(V_PASSES, i, 0)
-            finish(i - 4, 0)
-            if i % 2 == 1:
-                next_quantize()
-                next_group(MID_VECTOR_COLS)
+        next_quantize()
+        next_group(MID_VECTOR_COLS)
+        finish(4, 0)
+
+        def prepare():
+            next_quantize()
+            next_group(LATE_VECTOR_COLS)
 
         for j in range(1, CHUNKS):
-            for g in ZETA_PASSES:
+            sweep(0, low, j)
+            prepare()
+            for g in (1, 2, 3):
                 sweep(g, low, j)
                 finish(4 + g, j - 1)
-                if g % 2 == 0:
-                    next_quantize()
-                    next_group(LATE_VECTOR_COLS)
-            for i in low:
-                tile_passes(ZETA_PASSES, 4 + i, j)
+            prepare()
+            tile_passes(ZETA_PASSES, 4, j)
+            tile_passes(ZETA_PASSES, 5, j)
+            for i in (0, 1, 2):
                 add_beta(i, j)
-                if i > 0:
-                    tile_passes(V_PASSES, i - 1, j)
-                    add_beta(3 + i, j)
-                    finish(i - 1, j)
-                next_quantize()
-                next_group(LATE_VECTOR_COLS)
-            add_beta(7, j)
-            for i in (3, 4, 5, 6, 7):
+            prepare()
+            add_beta(3, j)
+            add_beta(4, j)
+            for i in (0, 1):
                 tile_passes(V_PASSES, i, j)
-                if i == 3 or j == CHUNKS - 1:
-                    finish(i, j)
+                finish(i, j)
+            prepare()
+            tile_passes(ZETA_PASSES, 6, j)
+            add_beta(5, j)
+            add_beta(6, j)
+            prepare()
+            for i in (2, 3, 4):
+                tile_passes(V_PASSES, i, j)
+                finish(i, j)
+            prepare()
+            tile_passes(ZETA_PASSES, 7, j)
+            add_beta(7, j)
+            for i in (5, 6, 7):
+                tile_passes(V_PASSES, i, j)
+        for i in (5, 6, 7):
+            finish(i, CHUNKS - 1)

@@ -26,7 +26,7 @@ V_PASSES = (4, 5)
 EARLY_VECTOR_COLS = 512
 MID_VECTOR_COLS = 160
 LATE_VECTOR_COLS = 0
-WARM = (7, 2, 8)
+WARM = (0, 0, 0)
 WARM_N = 256
 RAW_BUFS = 8
 

from contextlib import ExitStack

import concourse.mybir as mybir
from concourse.masks import make_identity

X, Y, C = 1024, 1536, 512
FLOPS = 2 * X * Y * (X + C + Y)

F32 = mybir.dt.float32
BF16 = mybir.dt.bfloat16
U32 = mybir.dt.uint32
U8 = mybir.dt.uint8
E4M3 = mybir.dt.float8_e4m3fn_x4
E5M2 = mybir.dt.float8_e5m2_x4
ADD = mybir.AluOpType.add
MULT = mybir.AluOpType.mult

P = 128
PACK = 4
K_PASS = P * PACK
N_TILE = 512
ROW_TILES = X // P
CHUNKS = Y // N_TILE
ZETA_PASSES = (0, 1, 2, 3)
V_PASSES = (4, 5)
EARLY_VECTOR_COLS = 512
MID_VECTOR_COLS = 160
LATE_VECTOR_COLS = 0
WARM = (0, 0, 0)
WARM_N = 256
RAW_BUFS = 8


def tile_meridional_vorticity_advection_s2_kernel(
    tc, d_x, psi, background, d_coarse, cores, d_fine, beta, out
):
    nc = tc.nc
    left_of = [(background, 0, E4M3), (cores, 0, E5M2), (cores, 1, E5M2), (cores, 2, E5M2), (d_x, 0, E4M3), (d_x, 1, E4M3)]
    right_of = [(d_coarse, 0), (d_fine, 0), (d_fine, 1), (d_fine, 2), (psi, 0), (psi, 1)]
    out_rows = out.rearrange("(p i) y -> p i y", i=ROW_TILES)

    with ExitStack() as ctx:
        keep = ctx.enter_context(tc.tile_pool(name="keep", bufs=1))
        stream = ctx.enter_context(tc.tile_pool(name="stream", bufs=1))
        psum = ctx.enter_context(tc.psum_pool(name="psum", bufs=1))
        ctx.enter_context(tc.manual_schedule())

        free_banks = list(range(8))
        left_raw, left_grouped, left_mx = {}, {}, {}
        right_raw, right_grouped, right_mx = {}, {}, {}
        open_banks, shifted = {}, {}

        def take_bank(shape):
            b = free_banks.pop(0)
            return b, psum.tile(shape, F32, name="bank%d" % b)

        ident = keep.tile([P, P], F32, name="ident")
        make_identity(nc, ident[:])
        beta_cols = keep.tile([P, 2, 6], BF16, name="beta_cols")
        beta_row = keep.tile([P, Y], BF16, name="beta_row")

        def load_beta():
            nc.sync.dma_start(out=beta_cols[:], in_=beta.rearrange("(h p c) -> p h c", h=2, c=6))

        def spread_beta():
            words = beta_cols[:].rearrange("p h c -> p (h c)").bitcast(F32)
            row_words = beta_row[:].bitcast(F32)
            for h in range(2):
                b, bank = take_bank([P, 3, P])
                for c in range(3):
                    column = words[:, 3 * h + c : 3 * h + c + 1].to_broadcast([P, P])
                    nc.tensor.transpose(bank[:, c, :], column, ident[:])
                nc.scalar.copy(
                    out=row_words[:, 3 * P * h : 3 * P * (h + 1)].rearrange("p (n c) -> p n c", c=3),
                    in_=bank[:].rearrange("p c n -> p n c"),
                )
                free_banks.append(b)

        def load_left(first_pass, pairs):
            matrix = left_of[first_pass][0]
            k = matrix.shape[1]
            rows = matrix.rearrange("(p i) k -> p (i k)", i=ROW_TILES)
            raw = keep.tile([P, 2 * k * len(pairs)], BF16, name="left_raw%d_%d" % (first_pass, pairs[0]))
            nc.sync.dma_start(out=raw[:], in_=rows[:, 2 * k * pairs[0] : 2 * k * (pairs[-1] + 1)])
            for n, pair in enumerate(pairs):
                for g in range(k // K_PASS):
                    left_raw[first_pass + g, pair] = (raw[:].bitcast(F32), n * k + g * (K_PASS // 2), k // 2)

        def turn_left(*units):
            grouped = stream.tile([P, 4 * K_PASS], BF16, name="left_grouped", bufs=4, align_bytes=64)
            for n, (g, pair) in enumerate(units):
                words, first, tile_words = left_raw[g, pair]
                b, bank = take_bank([P, 2, 2, P])
                for s in range(2):
                    for u in range(2):
                        w0 = first + s * tile_words
                        nc.tensor.transpose(bank[:, s, u, :], words[:, w0 + u : w0 + K_PASS // 2 : 2], ident[:])
                nc.scalar.copy(
                    out=grouped[:, 2 * K_PASS * n : 2 * K_PASS * (n + 1)]
                    .bitcast(F32)
                    .rearrange("p (s r u) -> p s r u", s=2, u=2),
                    in_=bank[:].rearrange("p s u r -> p s r u"),
                )
                free_banks.append(b)
            left_grouped[units] = grouped

        def quantize_left(*units):
            width = 2 * P * len(units)
            codes = keep.tile([P, width], U32, name="left_codes%d_%d" % units[0], align_bytes=64)
            scales = keep.tile([P, width], U8, name="left_scales%d_%d" % units[0], align_bytes=64)
            nc.vector.quantize_mx(
                out=codes[:].bitcast(left_of[units[0][0]][2]),
                scales=scales[:],
                in_=left_grouped[units][:, : PACK * width],
            )
            for n, unit in enumerate(units):
                left_mx[unit] = (codes, scales, 2 * P * n)

        def load_right(g, j):
            matrix, part = right_of[g]
            rows = matrix[part * K_PASS : (part + 1) * K_PASS, j * N_TILE : (j + 1) * N_TILE]
            raw = stream.tile([P, PACK, N_TILE], BF16, name="right_raw", bufs=RAW_BUFS)
            nc.sync.dma_start(out=raw[:], in_=rows.rearrange("(p t) n -> p t n", t=PACK))
            right_raw[g, j] = raw

        def group_right(g, j, vector_cols):
            raw = right_raw[g, j]
            grouped = stream.tile([P, N_TILE, PACK], BF16, name="right_grouped", bufs=4, align_bytes=64)
            split = N_TILE - vector_cols
            if split > 0:
                nc.scalar.copy(
                    out=grouped[:, :split, :].rearrange("p (c i) t -> p c t i", i=4),
                    in_=raw[:, :, :split].rearrange("p t (c i) -> p c t i", i=4),
                )
            if vector_cols > 0:
                nc.vector.tensor_copy(
                    out=grouped[:, split:, :].rearrange("p (c i) t -> p c t i", i=4),
                    in_=raw[:, :, split:].rearrange("p t (c i) -> p c t i", i=4),
                )
            right_grouped[g, j] = grouped

        def quantize_right(g, j):
            codes = keep.tile([P, N_TILE], U32, name="right_codes%d_%d" % (g, j), align_bytes=64)
            scales = keep.tile([P, N_TILE], U8, name="right_scales%d_%d" % (g, j), align_bytes=64)
            nc.vector.quantize_mx(
                out=codes[:].bitcast(E4M3),
                scales=scales[:],
                in_=right_grouped[g, j][:].rearrange("p n t -> p (n t)"),
            )
            right_mx[g, j] = (codes, scales)

        def multiply(g, i, j):
            passes = ZETA_PASSES if g in ZETA_PASSES else V_PASSES
            if g == passes[0]:
                open_banks[i] = take_bank([P, N_TILE])
            left_codes, left_scales, first = left_mx[g, i // 2]
            right_codes, right_scales = right_mx[g, j]
            cols = slice(first + P * (i % 2), first + P * (i % 2 + 1))
            nc.tensor.matmul_mx(
                out=open_banks[i][1][:],
                lhsT=left_codes[:, cols].bitcast(left_of[g][2]),
                lhsT_scale=left_scales[:, cols],
                rhs=right_codes[:].bitcast(E4M3),
                rhs_scale=right_scales[:],
                start=(g == passes[0]),
                stop=(g == passes[-1]),
            )

        def add_beta(i, j):
            b, bank = open_banks[i]
            shifted[i] = stream.tile([P, N_TILE], F32, name="shifted", bufs=12)
            nc.vector.tensor_tensor(
                out=shifted[i][:], in0=bank[:], in1=beta_row[:, j * N_TILE : (j + 1) * N_TILE], op=ADD
            )
            free_banks.append(b)

        def finish(i, j):
            b, bank = open_banks[i]
            nc.vector.tensor_tensor(out=shifted[i][:], in0=bank[:], in1=shifted[i][:], op=MULT)
            free_banks.append(b)
            nc.sync.dma_start(out=out_rows[:, i, j * N_TILE : (j + 1) * N_TILE], in_=shifted[i][:])

        warm_in = keep.tile([P, PACK * WARM_N], BF16, name="warm_in", align_bytes=64)
        warm_codes = keep.tile([P, WARM_N], U32, name="warm_codes", align_bytes=64)
        warm_scales = keep.tile([P, WARM_N], U8, name="warm_scales", align_bytes=64)

        def warm_up(count):
            if count == 0:
                return
            b, bank = take_bank([P, WARM_N])
            for n in range(count):
                nc.tensor.matmul_mx(
                    out=bank[:],
                    lhsT=warm_codes[:, :P].bitcast(E4M3),
                    lhsT_scale=warm_scales[:, :P],
                    rhs=warm_codes[:].bitcast(E4M3),
                    rhs_scale=warm_scales[:],
                    start=True,
                    stop=True,
                )
            free_banks.append(b)

        if sum(WARM):
            nc.vector.memset(warm_in[:].bitcast(U32), 0)
            nc.vector.quantize_mx(out=warm_codes[:].bitcast(E4M3), scales=warm_scales[:], in_=warm_in[:])

        low, high = range(0, 4), range(4, 8)

        def sweep(g, tiles, j):
            for i in tiles:
                multiply(g, i, j)

        load_left(0, [0, 1])
        load_beta()
        load_left(1, [0])
        load_right(0, 0)
        load_left(1, [1])
        load_right(1, 0)
        load_left(0, [2, 3])
        load_right(2, 0)
        load_left(1, [2])
        load_right(3, 0)
        load_left(1, [3])
        load_right(4, 0)
        load_right(5, 0)
        load_left(4, [0])
        load_left(4, [1])
        load_left(4, [2])
        load_left(4, [3])

        later = [(g, j) for j in range(1, CHUNKS) for g in range(6)]
        to_load = list(later)
        to_group = [(4, 0), (5, 0)] + later
        to_quantize = list(to_group)

        def next_load():
            if to_load:
                load_right(*to_load.pop(0))

        def next_group(cols):
            if to_group:
                group_right(*to_group.pop(0), cols)
                next_load()

        def next_quantize():
            if to_quantize:
                quantize_right(*to_quantize.pop(0))

        def tile_passes(passes, i, j):
            for g in passes:
                multiply(g, i, j)

        def turn_cores(pair):
            turn_left((1, pair), (2, pair))
            turn_left((3, pair))

        for n in range(RAW_BUFS - 6):
            next_load()

        warm_up(WARM[0])
        turn_left((0, 0), (0, 1))
        spread_beta()
        warm_up(WARM[1])
        quantize_left((0, 0), (0, 1))
        turn_cores(0)
        warm_up(WARM[2])
        group_right(0, 0, EARLY_VECTOR_COLS)
        next_load()
        quantize_left((1, 0), (2, 0))
        quantize_right(0, 0)
        quantize_left((3, 0))
        turn_cores(1)
        sweep(0, low, 0)
        group_right(1, 0, EARLY_VECTOR_COLS)
        next_load()
        quantize_left((1, 1), (2, 1))
        quantize_right(1, 0)
        quantize_left((3, 1))
        turn_left((0, 2), (0, 3))
        sweep(1, low, 0)
        group_right(2, 0, EARLY_VECTOR_COLS)
        next_load()
        quantize_left((0, 2), (0, 3))
        quantize_right(2, 0)
        turn_cores(2)
        sweep(2, low, 0)
        group_right(3, 0, EARLY_VECTOR_COLS)
        next_load()
        quantize_left((1, 2), (2, 2))
        quantize_right(3, 0)
        quantize_left((3, 2))
        turn_cores(3)
        sweep(3, low, 0)
        next_group(MID_VECTOR_COLS)
        add_beta(0, 0)
        quantize_left((1, 3), (2, 3))
        add_beta(1, 0)
        quantize_left((3, 3))
        for i in (4, 5):
            tile_passes(ZETA_PASSES, i, 0)
        add_beta(2, 0)
        add_beta(3, 0)
        next_quantize()
        next_group(MID_VECTOR_COLS)
        turn_left((4, 0), (5, 0))
        turn_left((4, 1), (5, 1))
        add_beta(4, 0)
        add_beta(5, 0)
        for i in (6, 7):
            tile_passes(ZETA_PASSES, i, 0)
        next_quantize()
        quantize_left((4, 0), (5, 0))
        next_group(MID_VECTOR_COLS)
        quantize_left((4, 1), (5, 1))
        add_beta(6, 0)
        add_beta(7, 0)
        next_quantize()
        next_group(MID_VECTOR_COLS)
        turn_left((4, 2), (5, 2))
        turn_left((4, 3), (5, 3))
        for i in low:
            tile_passes(V_PASSES, i, 0)
        next_quantize()
        next_group(MID_VECTOR_COLS)
        finish(0, 0)
        quantize_left((4, 2), (5, 2))
        finish(1, 0)
        quantize_left((4, 3), (5, 3))
        finish(2, 0)
        finish(3, 0)
        for i in high:
            tile_passes(V_PASSES, i, 0)
        next_quantize()
        next_group(MID_VECTOR_COLS)
        finish(4, 0)

        def prepare():
            next_quantize()
            next_group(LATE_VECTOR_COLS)

        for j in range(1, CHUNKS):
            sweep(0, low, j)
            prepare()
            for g in (1, 2, 3):
                sweep(g, low, j)
                finish(4 + g, j - 1)
            prepare()
            tile_passes(ZETA_PASSES, 4, j)
            tile_passes(ZETA_PASSES, 5, j)
            for i in (0, 1, 2):
                add_beta(i, j)
            prepare()
            add_beta(3, j)
            add_beta(4, j)
            for i in (0, 1):
                tile_passes(V_PASSES, i, j)
                finish(i, j)
            prepare()
            tile_passes(ZETA_PASSES, 6, j)
            add_beta(5, j)
            add_beta(6, j)
            prepare()
            for i in (2, 3, 4):
                tile_passes(V_PASSES, i, j)
                finish(i, j)
            prepare()
            tile_passes(ZETA_PASSES, 7, j)
            add_beta(7, j)
            for i in (5, 6, 7):
                tile_passes(V_PASSES, i, j)
        for i in (5, 6, 7):
            finish(i, CHUNKS - 1)
